import numpy as np
import ml_dtypes


def mxq(x, axis, fmt="e4m3"):
    dtype, down = {"e4m3": (ml_dtypes.float8_e4m3fn, 7), "e5m2": (ml_dtypes.float8_e5m2, 14)}[fmt]
    v = np.moveaxis(np.asarray(x, np.float32).astype(ml_dtypes.bfloat16).astype(np.float64), axis, -1)
    blocks = v.reshape(v.shape[:-1] + (-1, 32))
    amax = np.abs(blocks).max(-1, keepdims=True)
    byte = np.maximum(np.where(amax > 0, np.frexp(amax)[1] - 1 + 127, 0) - down, 1)
    scale = np.exp2(byte - 127.0)
    codes = (blocks / scale).astype(np.float32).astype(dtype).astype(np.float64)
    return np.moveaxis((codes * scale).reshape(v.shape), -1, axis)


WIDE = False


def mx_kscale(k):
    if not WIDE:
        return np.ones(k)
    levels = np.array([10, -10, 5, -5, 0])
    if k % 512:
        return np.exp2(np.random.permutation(np.resize(levels, k // 32))).repeat(32)
    a = np.empty((k // 512, 16))
    for p in range(k // 512):
        a[p, :8] = np.random.permutation(np.resize(levels, 8))
        for g in range(8):
            far = levels[np.abs(levels - a[p, g]) >= 10]
            a[p, g + 8] = far[np.random.randint(len(far))]
    return np.exp2(a.ravel()).repeat(32)


BF16 = ml_dtypes.bfloat16


def bf(x):
    return np.asarray(x, np.float32).astype(BF16)


def f64(x):
    return np.asarray(x).astype(np.float64)

E4M3FN = np.array([(-1.0 if i & 128 else 1.0) * ((1.0 + (i & 7) / 8.0) * 2.0 ** (((i >> 3) & 15) - 7) if i & 120 else (i & 7) * 2.0 ** -9) for i in range(256)])


def e4m3fn_bytes(y):
    return np.clip(np.asarray(y, np.float64), -448.0, 448.0).astype(np.float32).astype(ml_dtypes.float8_e4m3fn).view(np.uint8)


def e4m3fn_values(b):
    return E4M3FN[b]


B, D, G = 2048, 1024, 128


def setup_inputs():
    s = mx_kscale(B)
    common = np.tile(np.random.standard_normal((B, G)), (1, D // G))
    za = (np.sqrt(0.6) * common + np.sqrt(0.4) * np.random.standard_normal((B, D))) / np.sqrt(B) * s[:, None]
    zb = (np.sqrt(0.6) * common + np.sqrt(0.4) * np.random.standard_normal((B, D))) / np.sqrt(B) / s[:, None]
    za_scale = (np.abs(za).reshape(B, D // G, G).max(axis=2) / 448.0).astype(np.float32)
    za_bytes = e4m3fn_bytes(za / np.repeat(f64(za_scale), G, axis=1))
    return {"za_bytes": za_bytes,
            "za_scale": za_scale,
            "zb": bf(zb)}


def reference(za_bytes, za_scale, zb):
    za = e4m3fn_values(za_bytes) * np.repeat(f64(za_scale), G, axis=1)
    c = mxq(za, 0, "e4m3").T @ mxq(f64(zb), 0, "e4m3")
    d = c - np.eye(D)
    loss = np.square(d).sum(axis=1)
    return loss, d

from contextlib import ExitStack

import concourse.mybir as mybir
from concourse.masks import make_identity

B, D, G = 2048, 1024, 128
FLOPS = 2 * B * D * D + 3 * D * D

F32 = mybir.dt.float32
BF16 = mybir.dt.bfloat16
U32 = mybir.dt.uint32
U8 = mybir.dt.uint8
FP8 = mybir.dt.float8_e4m3fn
FP8X4 = mybir.dt.float8_e4m3fn_x4
ACT = mybir.ActivationFunctionType
ALU = mybir.AluOpType

P = 128
PACK = 4
K_PASS = P * PACK
PASSES = B // K_PASS
MT = D // P
NW = 512
NH = D // NW

LOADS = "b00 a0 b01 b10 a2 b11 b20 a3l a1l b21 a3r a1r b30 b31"
SEQ = (
    "WS50 WS20 WS40 WS70 IB00 WS00 WV30 WS10 WS52 WS22 WS32 WS62 QB00 WS42 "
    "WV60 WS33 WS31 WS21 IB01 IB10 QB01 QB10 WS01 WS12 WS63 WV02 IB11 IB20 "
    "WS61 QB11 QB20 IA3 F71 IB21 WS43 QA3 QB21 WS41 WS71 WS51 IA6 WS73 "
    "WS72 WS53 IB30 QA6 F10 IA4 QB30 WS23 WS11 QA4 WS03 IB31 IA7 F51 "
    "WS13 ES60 ES30 QB31 QA7 F30 HS60 ES41 ES40 ES61 IA5 F41 ES31 QA5 "
    "ES70 HS30 IA0 EV71 QA0 IA1 HS70 ES50 F61 HS50 QA1 IA2 HS41 ES00 "
    "HS31 ES01 F00 QA2 HS61 F20 EV10 EV51 HS71 HS01 ES11 HS10 HS11 ES21 "
    "HV00 EV20 HV40 HV20 HV21 HS51 "
)


def tile_cross_view_redundancy_loss_d1_kernel(tc, za_bytes, za_scale, zb, out_0, out_1):
    nc = tc.nc
    with ExitStack() as ctx:
        keep = ctx.enter_context(tc.tile_pool(name="keep", bufs=1))
        stage = ctx.enter_context(tc.tile_pool(name="stage", bufs=8))
        devp = ctx.enter_context(tc.tile_pool(name="devp", bufs=16))
        junkp = ctx.enter_context(tc.tile_pool(name="junkp", bufs=2))
        pacc = ctx.enter_context(tc.psum_pool(name="pacc", bufs=8))
        ctx.enter_context(tc.manual_schedule())

        sc = keep.tile([P, PASSES, PACK * MT], F32, name="sc")
        za8 = [keep.tile([P, PACK, D], U8, name="za8_%d" % g) for g in range(PASSES)]
        zbr = [[keep.tile([P, PACK, NW], BF16, name="zbr_%d_%d" % (g, n)) for n in range(NH)] for g in range(PASSES)]
        wide = [keep.tile([P, PACK, PASSES, P], BF16, name="wide_%d" % m) for m in range(MT)]
        bq = [[keep.tile([P, NW], U32, name="bq_%d_%d" % (g, n), align_bytes=64) for n in range(NH)] for g in range(PASSES)]
        bs = [[keep.tile([P, NW], U8, name="bs_%d_%d" % (g, n), align_bytes=64) for n in range(NH)] for g in range(PASSES)]
        aq = [keep.tile([P, PASSES, P], U32, name="aq_%d" % m, align_bytes=64) for m in range(MT)]
        asc = [keep.tile([P, PASSES, P], U8, name="as_%d" % m, align_bytes=64) for m in range(MT)]
        eye = keep.tile([P, 7 * P], F32, name="eye")
        loss = [keep.tile([P, P], F32, name="loss_%d" % n) for n in range(NH)]

        nc.scalar.dma_start(out=sc[:], in_=za_scale.rearrange("(g p t) m -> p g (t m)", p=P, t=PACK))

        za_v = za_bytes.rearrange("(g p t) i -> g p t i", p=P, t=PACK)
        zb_v = zb.rearrange("(g p t) j -> g p t j", p=P, t=PACK)

        for x in LOADS.split(" "):
            g = int(x[1])
            if x[0] == "b":
                n = int(x[2])
                nc.sync.dma_start(out=zbr[g][n][:], in_=zb_v[g][:, :, n * NW : (n + 1) * NW])
            elif len(x) == 2:
                nc.sync.dma_start(out=za8[g][:], in_=za_v[g])
            else:
                h = 0 if x[2] == "l" else 4 * P
                nc.sync.dma_start(out=za8[g][:, :, h : h + 4 * P], in_=za_v[g][:, :, h : h + 4 * P])

        nc.gpsimd.memset(eye[:], 0.0)
        make_identity(nc, eye[:, 3 * P : 4 * P])
        nc.gpsimd.memset(loss[0][:], 0.0)
        nc.gpsimd.memset(loss[1][:], 0.0)

        def widen(e, m, g):
            for t in range(PACK):
                dst = wide[m][:, t, g, :]
                src = za8[g][:, t, m * P : (m + 1) * P].bitcast(FP8)
                s = sc[:, g, t * MT + m : t * MT + m + 1]
                if e == "V":
                    nc.vector.tensor_scalar(out=dst, in0=src, scalar1=s, scalar2=None, op0=ALU.mult)
                else:
                    nc.scalar.activation(out=dst, in_=src, func=ACT.Copy, scale=s)

        il = {}

        def interleave(u):
            t = stage.tile([P, NW, PACK], BF16, name="il", align_bytes=64)
            il[u] = t
            src = zbr[int(u[1])][int(u[2])][:] if u[0] == "B" else wide[int(u[1])][:].rearrange("p t g c -> p t (g c)")
            nc.vector.tensor_copy(
                out=t[:].rearrange("p (c i) t -> p c t i", i=4),
                in_=src.rearrange("p t (c i) -> p c t i", i=4),
            )

        def quantize(u):
            if u[0] == "B":
                q, s = bq[int(u[1])][int(u[2])][:], bs[int(u[1])][int(u[2])][:]
            else:
                q = aq[int(u[1])][:].rearrange("p g c -> p (g c)")
                s = asc[int(u[1])][:].rearrange("p g c -> p (g c)")
            nc.vector.quantize_mx(out=q.bitcast(FP8X4), scales=s, in_=il[u][:].rearrange("p n t -> p (n t)"))

        acc = {}
        dev = {}

        def matmul(m, n, g):
            if g == 0:
                acc[m, n] = pacc.tile([P, NW], F32, name="acc")
            nc.tensor.matmul_mx(
                out=acc[m, n][:],
                lhsT=aq[m][:, g, :].bitcast(FP8X4),
                lhsT_scale=asc[m][:, g, :],
                rhs=bq[g][n][:].bitcast(FP8X4),
                rhs_scale=bs[g][n][:],
                start=(g == 0),
                stop=(g == PASSES - 1),
            )

        def store(m, n):
            nc.sync.dma_start(out=out_1[m * P : (m + 1) * P, n * NW : (n + 1) * NW], in_=dev[m, n][:])

        by_scalar = set()

        def deviation(e, m, n):
            d = devp.tile([P, NW], F32, name="dev")
            dev[m, n] = d
            diagonal = n == m // 4
            q = m % 4
            if e == "S":
                nc.scalar.copy(out=d[:], in_=acc[m, n][:])
                by_scalar.add((m, n))
            elif diagonal:
                nc.vector.tensor_tensor(out=d[:], in0=acc[m, n][:], in1=eye[:, (3 - q) * P : (3 - q) * P + NW], op=ALU.subtract)
            else:
                nc.vector.tensor_copy(out=d[:], in_=acc[m, n][:])
            if e == "V" or not diagonal:
                store(m, n)

        def fix(m, n):
            if (m, n) in by_scalar:
                blk = dev[m, n][:, (m % 4) * P : (m % 4 + 1) * P]
                nc.vector.tensor_tensor(out=blk, in0=blk, in1=eye[:, 3 * P : 4 * P], op=ALU.subtract)
                store(m, n)

        def square(e, m, n):
            d = dev[m, n]
            dst = loss[n][:, m : m + 1]
            if e == "V":
                junk = junkp.tile([P, NW], F32, name="junk_v")
                nc.vector.scalar_tensor_tensor(out=junk[:], in0=d[:], scalar=1.0, in1=d[:], op0=ALU.mult, op1=ALU.mult, accum_out=dst)
            else:
                junk = junkp.tile([P, NW], F32, name="junk_s")
                nc.scalar.activation(out=junk[:], in_=d[:], func=ACT.Square, accum_out=dst)

        done_a = []
        done_b = []
        for tok in SEQ.split():
            k = tok[0]
            e = tok[1]
            if k == "W":
                widen(e, int(tok[2]), int(tok[3]))
            elif k == "I":
                interleave(tok[1:])
            elif k == "Q":
                quantize(tok[1:])
                if e == "B":
                    done_b.append((int(tok[2]), int(tok[3])))
                    for m in done_a:
                        matmul(m, int(tok[3]), int(tok[2]))
                else:
                    done_a.append(int(tok[2]))
                    for n in range(NH):
                        for g in range(PASSES):
                            if (g, n) in done_b:
                                matmul(int(tok[2]), n, g)
            elif k == "E":
                deviation(e, int(tok[2]), int(tok[3]))
            elif k == "F":
                fix(int(tok[1]), int(tok[2]))
            else:
                square(e, int(tok[2]), int(tok[3]))

        lt = pacc.tile([P, NW], F32, name="acc")
        for n in range(NH):
            nc.tensor.matmul(lt[:, 0:P], lhsT=loss[n][:], rhs=eye[:, 3 * P : 4 * P], is_transpose=True, start=(n == 0), stop=(n == NH - 1))
        lrow = keep.tile([MT, P], F32, name="lrow")
        nc.vector.tensor_copy(out=lrow[:], in_=lt[0:MT, 0:P])
        nc.sync.dma_start(out=out_0.rearrange("(m p) -> m p", p=P), in_=lrow[:])
